import numpy as np
import ml_dtypes


def mxq(x, axis, fmt="e4m3"):
    dtype, down = {"e4m3": (ml_dtypes.float8_e4m3fn, 7), "e5m2": (ml_dtypes.float8_e5m2, 14)}[fmt]
    v = np.moveaxis(np.asarray(x, np.float32).astype(ml_dtypes.bfloat16).astype(np.float64), axis, -1)
    blocks = v.reshape(v.shape[:-1] + (-1, 32))
    amax = np.abs(blocks).max(-1, keepdims=True)
    byte = np.maximum(np.where(amax > 0, np.frexp(amax)[1] - 1 + 127, 0) - down, 1)
    scale = np.exp2(byte - 127.0)
    codes = (blocks / scale).astype(np.float32).astype(dtype).astype(np.float64)
    return np.moveaxis((codes * scale).reshape(v.shape), -1, axis)


WIDE = False


def mx_kscale(k):
    if not WIDE:
        return np.ones(k)
    levels = np.array([10, -10, 5, -5, 0])
    if k % 512:
        return np.exp2(np.random.permutation(np.resize(levels, k // 32))).repeat(32)
    a = np.empty((k // 512, 16))
    for p in range(k // 512):
        a[p, :8] = np.random.permutation(np.resize(levels, 8))
        for g in range(8):
            far = levels[np.abs(levels - a[p, g]) >= 10]
            a[p, g + 8] = far[np.random.randint(len(far))]
    return np.exp2(a.ravel()).repeat(32)


def f64(x):
    return np.asarray(x).astype(np.float64)


def striped(idx):
    return np.tile(idx.reshape(-1, 16).T, (8, 1)).astype(np.uint16)


def unstriped(offs):
    return offs[:16].T.reshape(-1).astype(np.int64)


E2M1 = np.array([0.0, 0.5, 1.0, 1.5, 2.0, 3.0, 4.0, 6.0, -0.0, -0.5, -1.0, -1.5, -2.0, -3.0, -4.0, -6.0])


def pack_weight(w, fmt):
    k, n = w.shape
    w = f64(np.asarray(w, np.float32).astype(ml_dtypes.bfloat16)).reshape(k // 32, 32, n)
    amax = np.abs(w).max(1)
    if fmt == "e4m3":
        byte = np.frexp(amax)[1] - 1 + 127 - 7
    else:
        mant, ex = np.frexp(amax / 6.0)
        byte = np.where(mant > 0.5, ex, ex - 1) + 127
    byte = np.clip(np.where(amax > 0, byte, 1), 1, 254)
    scaled = (w * np.exp2(127.0 - byte)[:, None, :]).reshape(k, n).astype(np.float32)
    by_word = np.ascontiguousarray(scaled.reshape(k // 512, 128, 4, n).transpose(0, 1, 3, 2))
    if fmt == "e4m3":
        words = by_word.astype(ml_dtypes.float8_e4m3fn).view(np.uint8)
    else:
        c = by_word.astype(ml_dtypes.float4_e2m1fn).view(np.uint8) & 0xF
        words = (c[..., 0::2] | (c[..., 1::2] << 4)).reshape(k // 512, 128, 2 * n)
    return np.ascontiguousarray(words), np.ascontiguousarray(byte.astype(np.uint8).reshape(k // 512, 16, n))


def unpack_weight(words, scales, fmt):
    g, _, n = scales.shape
    words = np.ascontiguousarray(words).reshape(g, 128, n, -1)
    if fmt == "e4m3":
        vals = words.view(ml_dtypes.float8_e4m3fn).astype(np.float64)
    else:
        nib = np.empty((g, 128, n, 4), np.uint8)
        nib[..., 0::2] = words & 0xF
        nib[..., 1::2] = words >> 4
        vals = E2M1[nib]
    vals = vals * np.repeat(np.exp2(scales.astype(np.float64) - 127.0), 8, axis=1)[..., None]
    return vals.transpose(0, 1, 3, 2).reshape(g * 512, n)


def gelu(v):
    return 0.5 * v * (1.0 + np.tanh(np.sqrt(2.0 / np.pi) * (v + 0.044715 * v**3)))


K, T, S, H, S2, T3, T2, P = 1024, 2048, 512, 1024, 1024, 2048, 1024, 512

def setup_inputs():
    n = np.random.standard_normal
    s = mx_kscale(K)[:, None]
    u = mx_kscale(H)[:, None]
    tab_words, tab_scales = pack_weight(n((K, T)) * s, "e4m3")
    tab2_words, tab2_scales = pack_weight(n((H, T3)) / np.sqrt(H) / u, "e4m3")
    w4_words, w4_scales = pack_weight(n((K, H)) / np.sqrt(K) / s, "e2m1")
    return {
        "tab_words": tab_words, "tab_scales": tab_scales,
        "offs": striped(np.random.permutation(T)[:S]),
        "tab2_words": tab2_words, "tab2_scales": tab2_scales,
        "offs2": striped(np.random.permutation(T3)[:S2]),
        "offs3": striped(np.random.permutation(T2)[:S]),
        "pos1": striped(np.random.permutation(T2)[:P]),
        "pos2": striped(np.random.permutation(T2)[:P]),
        "w1": (0.55 * n((K, H)) / np.sqrt(K) / s).astype(np.float32),
        "w4_words": w4_words, "w4_scales": w4_scales,
        "gain": (np.exp(0.3 * n(H)) * u[:, 0]).astype(np.float32),
        "wgs": np.exp(0.3 * n((128, S))).astype(np.float32),
        "page0": (n((H, T2)) * u).astype(np.float32),
        "sky": (0.6 * n((H, T2)) * u).astype(np.float32),
        "low": (0.8 * n((S2, P))).astype(np.float32),
    }

def reference(tab_words, tab_scales, offs, tab2_words, tab2_scales, offs2, offs3, pos1, pos2,
              w1, w4_words, w4_scales, gain, wgs, page0, sky, low):
    v = unpack_weight(tab_words, tab_scales, "e4m3")[:, unstriped(offs)]
    v2 = unpack_weight(tab2_words, tab2_scales, "e4m3")[:, unstriped(offs2)]
    w4 = unpack_weight(w4_words, w4_scales, "e2m1")
    a = mxq(f64(w1), 0, "e4m3").T @ v
    b = w4.T @ v
    h = f64(gain)[:, None] * (a + b * np.cos(a))
    page = f64(page0).copy()
    page[:, unstriped(offs3)] = np.tile(f64(wgs), (H // 128, 1)) * h
    x = mxq(page + f64(sky), 0, "e4m3")
    e = v2.T @ x
    arcs = e[:, unstriped(pos1)] - e[:, unstriped(pos2)]
    return np.maximum(arcs, f64(low))

@@ -1,0 +1,312 @@
+from contextlib import ExitStack
+
+import concourse.mybir as mybir
+from concourse.masks import make_identity
+
+K, T, S, H, S2, T3, T2, NP = 1024, 2048, 512, 1024, 1024, 2048, 1024, 512
+FLOPS = 2 * 2 * K * H * S + 2 * H * S2 * T2
+
+F32 = mybir.dt.float32
+BF16 = mybir.dt.bfloat16
+I32 = mybir.dt.int32
+U32 = mybir.dt.uint32
+U16 = mybir.dt.uint16
+U8 = mybir.dt.uint8
+FP8X4 = mybir.dt.float8_e4m3fn_x4
+FP4X4 = mybir.dt.float4_e2m1fn_x4
+ALU = mybir.AluOpType
+ACT = mybir.ActivationFunctionType
+
+P = 128
+PASSES = 2
+PAIR = 2 * P
+HALF = 512
+
+
+def tile_list_lens_arc_scores_kernel(
+    tc, tab_words, tab_scales, offs, tab2_words, tab2_scales, offs2, offs3, pos1, pos2,
+    w1, w4_words, w4_scales, gain, wgs, page0, sky, low, out,
+):
+    nc = tc.nc
+    with ExitStack() as ctx:
+        lists = ctx.enter_context(tc.tile_pool(name="lists", bufs=1))
+        sb = ctx.enter_context(tc.tile_pool(name="sb", bufs=1))
+        ps = ctx.enter_context(tc.psum_pool(name="ps", bufs=1))
+
+        def tile(shape, dtype, name, tag=None, bufs=1):
+            return sb.tile(shape, dtype, name=name, tag=tag or name, bufs=bufs, align_bytes=64)
+
+        def load_list(ap, name):
+            t = lists.tile(list(ap.shape), U16, name=name)
+            nc.sync.dma_start(t[:], ap)
+            return t
+
+        tab_sc = tile([P, PASSES * T], U8, "tab_sc")
+        nc.vector.memset(tab_sc[:].bitcast(I32), 0)
+        w4_sc = tile([P, PASSES * H], U8, "w4_sc")
+        nc.vector.memset(w4_sc[:].bitcast(I32), 0)
+        tab2_sc = tile([P, T3], U8, "tab2_sc")
+        nc.vector.memset(tab2_sc[:].bitcast(I32), 0)
+        ident = tile([P, P], F32, "ident")
+        make_identity(nc, ident[:])
+
+        idx = load_list(offs, "idx")
+        idx3 = load_list(offs3, "idx3")
+        p1 = load_list(pos1, "p1")
+        p2 = load_list(pos2, "p2")
+        idx2 = load_list(offs2, "idx2")
+
+        def load_words(words, a, name):
+            t = tile([P, T], U32, name, tag="words%d" % a)
+            nc.sync.dma_start(t[:].bitcast(I32), words[a].rearrange("p n t -> p (n t)").bitcast(I32))
+            return t
+
+        def load_scales_side_by_side(dst, scales):
+            for q in range(4):
+                nc.sync.dma_start(
+                    dst[32 * q : 32 * q + 4, :].bitcast(I32).rearrange("q (a t) -> q a t", a=PASSES),
+                    scales.bitcast(I32)[:, 4 * q : 4 * q + 4, :].rearrange("a q t -> q a t"),
+                )
+
+        w1_raw = {}
+
+        def load_w1(k):
+            for a in range(PASSES):
+                t = tile([P, 4, PAIR], F32, "w1_raw%d_%d" % (k, a))
+                src = w1[512 * a : 512 * (a + 1), PAIR * k : PAIR * (k + 1)]
+                nc.sync.dma_start(t[:], src.rearrange("(p j) c -> p j c", j=4))
+                w1_raw[k, a] = t
+
+        def load_w4(c0, c1, name):
+            t = tile([P, PASSES, 2 * (c1 - c0)], U8, name)
+            nc.sync.dma_start(
+                t[:].bitcast(I32),
+                w4_words.bitcast(I32)[:, :, c0 // 2 : c1 // 2].rearrange("a p c -> p a c"),
+            )
+            return t
+
+        page, sky_t = {}, {}
+
+        def load_rows(dst, src, k, name):
+            for i in (2 * k, 2 * k + 1):
+                t = tile([P, T2], F32, "%s%d" % (name, i))
+                nc.sync.dma_start(t[:], src[P * i : P * (i + 1), :])
+                dst[i] = t
+
+        tab_w = [load_words(tab_words, 0, "tab_w0")]
+        load_scales_side_by_side(tab_sc, tab_scales)
+        load_w1(0)
+        w4_first = load_w4(0, PAIR, "w4_first")
+        load_scales_side_by_side(w4_sc, w4_scales)
+        tab_w.append(load_words(tab_words, 1, "tab_w1"))
+        load_w1(1)
+        w4_rest = load_w4(PAIR, H, "w4_rest")
+        wgs_t = tile([P, S], F32, "wgs_t")
+        nc.sync.dma_start(wgs_t[:], wgs)
+        gain_t = tile([P, H // P], F32, "gain_t")
+        with nc.allow_non_contiguous_dma(reason="one gain value for each row, rows on partitions"):
+            nc.sync.dma_start(gain_t[:], gain.rearrange("(i p) -> p i", p=P))
+        load_rows(page, page0, 0, "page")
+        load_w1(2)
+        load_rows(sky_t, sky, 0, "sky")
+        load_rows(page, page0, 1, "page")
+        load_w1(3)
+        load_rows(sky_t, sky, 1, "sky")
+        for k in (2, 3):
+            load_rows(page, page0, k, "page")
+            load_rows(sky_t, sky, k, "sky")
+
+        v_w, v_s = [], []
+        for a in range(PASSES):
+            s_t = tile([P, S], U8, "v_s%d" % a)
+            nc.vector.tensor_copy(s_t[:], tab_sc[:, T * a : T * (a + 1)].indirect(idx[:]))
+            w_t = tile([P, S], U32, "v_w%d" % a)
+            nc.vector.tensor_copy(w_t[:], tab_w[a][:].indirect(idx[:]))
+            v_s.append(s_t)
+            v_w.append(w_t)
+
+        for q in range(4):
+            nc.sync.dma_start(
+                tab2_sc[32 * q : 32 * q + 8, :].bitcast(I32),
+                tab2_scales.bitcast(I32)[:, 4 * q : 4 * q + 4, :],
+            )
+        tab2_w = [load_words(tab2_words, a, "tab2_w%d" % a) for a in range(PASSES)]
+
+        w1_q = {}
+
+        def quantise_w1(k, cast):
+            for a in range(PASSES):
+                grouped = tile([P, 4 * PAIR], BF16, "w1_bf", bufs=4)
+                cast(
+                    grouped[:].rearrange("p (c i j) -> p c j i", i=4, j=4),
+                    w1_raw[k, a][:].rearrange("p j (c i) -> p c j i", i=4),
+                )
+                codes = tile([P, PAIR], U32, "w1_codes%d_%d" % (k, a))
+                scales = tile([P, PAIR], U8, "w1_scales%d_%d" % (k, a))
+                nc.vector.quantize_mx(codes[:].bitcast(FP8X4), scales[:], grouped[:])
+                w1_q[k, a] = (codes, scales)
+
+        def w4_operand(i, a):
+            if i < 2:
+                words = w4_first[:, a, 2 * P * i : 2 * P * (i + 1)]
+            else:
+                words = w4_rest[:, a, 2 * P * (i - 2) : 2 * P * (i - 1)]
+            return words.bitcast(FP4X4), w4_sc[:, H * a + P * i : H * a + P * (i + 1)]
+
+        acc_a, acc_b = {}, {}
+
+        def first_products(k):
+            for i in (2 * k, 2 * k + 1):
+                acc_a[i] = ps.tile([P, S], F32, name="acc_a%d" % (i % 2))
+                for a in range(PASSES):
+                    codes, scales = w1_q[k, a]
+                    cols = slice(P * (i % 2), P * (i % 2 + 1))
+                    nc.tensor.matmul_mx(
+                        acc_a[i][:], codes[:, cols].bitcast(FP8X4), scales[:, cols],
+                        v_w[a][:].bitcast(FP8X4), v_s[a][:], start=(a == 0), stop=(a == PASSES - 1),
+                    )
+            for i in (2 * k, 2 * k + 1):
+                acc_b[i] = ps.tile([P, S], F32, name="acc_b%d" % (i % 2))
+                for a in range(PASSES):
+                    words, scales = w4_operand(i, a)
+                    nc.tensor.matmul_mx(
+                        acc_b[i][:], words, scales,
+                        v_w[a][:].bitcast(FP8X4), v_s[a][:], start=(a == 0), stop=(a == PASSES - 1),
+                    )
+
+        h_tags = ["h_even", "h_odd"] * 3 + ["h6", "h7"]
+        h, factor = {}, {}
+
+        def features(k):
+            pair = (2 * k, 2 * k + 1)
+            sines = tile([P, 2 * S], F32, "sines")
+            squares = tile([P, 2 * S], F32, "squares")
+            for i in pair:
+                cols = slice(S * (i % 2), S * (i % 2 + 1))
+                nc.scalar.activation(sines[:, cols], acc_a[i][:], ACT.Sin, scale=0.5)
+                if k == 0:
+                    nc.scalar.activation(squares[:, cols], sines[:, cols], ACT.Square)
+            if k > 0:
+                nc.scalar.activation(squares[:], sines[:], ACT.Square)
+            factors = tile([P, 2 * S], F32, "factors")
+            u = {}
+            for i in pair:
+                cols = slice(S * (i % 2), S * (i % 2 + 1))
+                factor[i] = factors[:, cols]
+                nc.gpsimd.tensor_scalar(factor[i], wgs_t[:], gain_t[:, i : i + 1], 0.0, ALU.mult, ALU.add)
+                u[i] = tile([P, S], F32, "u%d" % (i % 2))
+                nc.vector.scalar_tensor_tensor(u[i][:], squares[:, cols], -0.5, acc_b[i][:], ALU.add, ALU.mult)
+            for i in pair:
+                h[i] = tile([P, S], F32, "h%d" % i, tag=h_tags[i])
+                nc.vector.scalar_tensor_tensor(h[i][:], u[i][:], -2.0, acc_a[i][:], ALU.mult, ALU.add)
+
+        def refresh(i):
+            nc.vector.tensor_tensor(page[i][:].indirect(idx3[:]), h[i][:], factor[i], ALU.mult)
+
+        x_turned, x_grouped, x_q = {}, {}, {}
+
+        def add_sky(i):
+            b, ii = divmod(i, 4)
+            for half in range(2):
+                if ii == 0:
+                    x_turned[b, half] = tile([P, 4 * HALF], BF16, "x_turned%d" % half)
+                bank = ps.tile([P, HALF], F32, name="turn", bufs=4)
+                for c in range(4):
+                    cols = slice(HALF * half + P * c, HALF * half + P * (c + 1))
+                    dst = bank[:, P * c : P * (c + 1)]
+                    nc.tensor.matmul(dst, sky_t[i][:, cols], ident[:], start=True, stop=False, is_transpose=True)
+                    nc.tensor.matmul(dst, page[i][:, cols], ident[:], start=False, stop=True, is_transpose=True)
+                dst = x_turned[b, half][:].rearrange("n (c u p e) -> n c u p e", c=4, u=2, e=2)
+                nc.scalar.copy(
+                    dst[:, :, :, 32 * ii : 32 * (ii + 1), :],
+                    bank[:].rearrange("n (c p u e) -> n c u p e", c=4, u=2, e=2),
+                )
+
+        def turn_back(b, half):
+            x_grouped[b, half] = tile([P, 4 * HALF], BF16, "x_grouped%d" % half)
+            pairs = x_turned[b, half][:].bitcast(F32)
+            dst = x_grouped[b, half][:].bitcast(F32)
+            for g in range(2):
+                bank = ps.tile([P, HALF], F32, name="turn", bufs=4)
+                for u in range(2):
+                    for c in range(2):
+                        first = P * (2 * (2 * g + c) + u)
+                        nc.tensor.transpose(
+                            bank[:, PAIR * u + P * c : PAIR * u + P * (c + 1)], pairs[:, first : first + P], ident[:]
+                        )
+                nc.scalar.copy(
+                    dst[:, HALF * g : HALF * (g + 1)].rearrange("p (n u) -> p n u", u=2),
+                    bank[:].rearrange("p (u n) -> p n u", u=2),
+                )
+
+        def quantise_x(b, half, tag):
+            codes = tile([P, HALF], U32, "x_codes%d_%d" % (b, half), tag=tag)
+            scales = tile([P, HALF], U8, "x_scales%d_%d" % (b, half))
+            nc.vector.quantize_mx(codes[:].bitcast(FP8X4), scales[:], x_grouped[b, half][:])
+            x_q[b, half] = (codes, scales)
+
+        quantise_w1(0, nc.scalar.copy)
+        first_products(0)
+        quantise_w1(1, nc.vector.tensor_copy)
+        for k in range(4):
+            features(k)
+            if k < 3:
+                first_products(k + 1)
+            if k < 2:
+                quantise_w1(k + 2, nc.scalar.copy)
+            for i in (2 * k, 2 * k + 1):
+                refresh(i)
+                if k == 2:
+                    quantise_x(0, i % 2, h_tags[i])
+            for i in (2 * k, 2 * k + 1):
+                add_sky(i)
+            if k % 2 == 1:
+                for half in range(2):
+                    turn_back(k // 2, half)
+
+        low_t = []
+        for m2 in range(4):
+            t = tile([P, 2, NP], F32, "low%d" % m2, tag="w1_raw%d_%d" % divmod(m2, 2))
+            nc.sync.dma_start(t[:], low[PAIR * m2 : PAIR * (m2 + 1), :].rearrange("(m p) j -> p m j", p=P))
+            low_t.append(t)
+
+        v2_s = tile([P, S2], U8, "v2_s", tag="h7")
+        nc.vector.tensor_copy(v2_s[:], tab2_sc[:].indirect(idx2[:]))
+
+        def gather_candidates(part, tag):
+            t = tile([P, PASSES * HALF], U32, "v2_w%d" % part, tag=tag)
+            for a in range(PASSES):
+                nc.vector.tensor_copy(
+                    t[:, HALF * a : HALF * (a + 1)], tab2_w[a][:].indirect(idx2[:, 32 * part : 32 * (part + 1)])
+                )
+            return t
+
+        v2_w = [gather_candidates(0, "factors")]
+        for half in range(2):
+            quantise_x(1, half, None)
+        v2_w.append(gather_candidates(1, "x_grouped1"))
+
+        for m in range(S2 // P):
+            scores = tile([P, T2], F32, "scores%d" % m, tag="sky%d" % m)
+            for half in range(2):
+                bank = ps.tile([P, HALF], F32, name="turn", bufs=4)
+                for a in range(PASSES):
+                    first = HALF * a + P * (m % 4)
+                    codes, scales = x_q[a, half]
+                    nc.tensor.matmul_mx(
+                        bank[:], v2_w[m // 4][:, first : first + P].bitcast(FP8X4),
+                        v2_s[4 * a : P, P * m : P * (m + 1)],
+                        codes[:].bitcast(FP8X4), scales[:], start=(a == 0), stop=(a == PASSES - 1),
+                    )
+                nc.scalar.copy(scores[:, HALF * half : HALF * (half + 1)], bank[:])
+            second = tile([P, NP], F32, "second", bufs=2)
+            arcs = tile([P, NP], F32, "arcs", bufs=2)
+            result = tile([P, NP], F32, "result", bufs=3)
+            parts = [(slice(16 * c, 16 * (c + 1)), slice(PAIR * c, PAIR * (c + 1))) for c in range(2)]
+            for entries, cols in parts:
+                nc.vector.tensor_copy(second[:, cols], scores[:].indirect(p2[:, entries]))
+            for entries, cols in parts:
+                nc.vector.tensor_tensor(arcs[:, cols], scores[:].indirect(p1[:, entries]), second[:, cols], ALU.subtract)
+            for entries, cols in parts:
+                nc.vector.tensor_tensor(result[:, cols], arcs[:, cols], low_t[m // 2][:, m % 2, cols], ALU.max)
+            nc.sync.dma_start(out[P * m : P * (m + 1), :], result[:])

@@ -42,19 +42,16 @@ def tile_list_lens_arc_scores_kernel(
             return t
 
         tab_sc = tile([P, PASSES * T], U8, "tab_sc")
-        nc.vector.memset(tab_sc[:].bitcast(I32), 0)
+        nc.gpsimd.memset(tab_sc[:, :T].bitcast(I32), 0)
+        nc.vector.memset(tab_sc[:, T:].bitcast(I32), 0)
         w4_sc = tile([P, PASSES * H], U8, "w4_sc")
         nc.vector.memset(w4_sc[:].bitcast(I32), 0)
         tab2_sc = tile([P, T3], U8, "tab2_sc")
         nc.vector.memset(tab2_sc[:].bitcast(I32), 0)
         ident = tile([P, P], F32, "ident")
         make_identity(nc, ident[:])
-
-        idx = load_list(offs, "idx")
-        idx3 = load_list(offs3, "idx3")
-        p1 = load_list(pos1, "p1")
-        p2 = load_list(pos2, "p2")
-        idx2 = load_list(offs2, "idx2")
+        gain_rows = tile([P, P], F32, "gain_rows")
+        nc.gpsimd.memset(gain_rows[:], 0.0)
 
         def load_words(words, a, name):
             t = tile([P, T], U32, name, tag="words%d" % a)
@@ -70,8 +67,8 @@ def tile_list_lens_arc_scores_kernel(
 
         w1_raw = {}
 
-        def load_w1(k):
-            for a in range(PASSES):
+        def load_w1(k, passes=(0, 1)):
+            for a in passes:
                 t = tile([P, 4, PAIR], F32, "w1_raw%d_%d" % (k, a))
                 src = w1[512 * a : 512 * (a + 1), PAIR * k : PAIR * (k + 1)]
                 nc.sync.dma_start(t[:], src.rearrange("(p j) c -> p j c", j=4))
@@ -87,64 +84,74 @@ def tile_list_lens_arc_scores_kernel(
 
         page, sky_t = {}, {}
 
-        def load_rows(dst, src, k, name):
-            for i in (2 * k, 2 * k + 1):
+        def load_rows(dst, src, tiles, name):
+            for i in tiles:
                 t = tile([P, T2], F32, "%s%d" % (name, i))
                 nc.sync.dma_start(t[:], src[P * i : P * (i + 1), :])
                 dst[i] = t
 
+        idx = load_list(offs, "idx")
         tab_w = [load_words(tab_words, 0, "tab_w0")]
         load_scales_side_by_side(tab_sc, tab_scales)
-        load_w1(0)
+        nc.sync.dma_start(gain_rows[: H // P, :], gain.rearrange("(i p) -> i p", p=P))
+        load_w1(0, (0,))
         w4_first = load_w4(0, PAIR, "w4_first")
-        load_scales_side_by_side(w4_sc, w4_scales)
+        load_w1(0, (1,))
         tab_w.append(load_words(tab_words, 1, "tab_w1"))
-        load_w1(1)
-        w4_rest = load_w4(PAIR, H, "w4_rest")
+        load_scales_side_by_side(w4_sc, w4_scales)
         wgs_t = tile([P, S], F32, "wgs_t")
         nc.sync.dma_start(wgs_t[:], wgs)
-        gain_t = tile([P, H // P], F32, "gain_t")
-        with nc.allow_non_contiguous_dma(reason="one gain value for each row, rows on partitions"):
-            nc.sync.dma_start(gain_t[:], gain.rearrange("(i p) -> p i", p=P))
-        load_rows(page, page0, 0, "page")
+        load_rows(page, page0, [0], "page")
+        idx3 = load_list(offs3, "idx3")
+        load_w1(1)
+        load_rows(page, page0, [1], "page")
+        w4_rest = load_w4(PAIR, H, "w4_rest")
         load_w1(2)
-        load_rows(sky_t, sky, 0, "sky")
-        load_rows(page, page0, 1, "page")
+        load_rows(sky_t, sky, [0, 1], "sky")
+        load_rows(page, page0, [2, 3], "page")
         load_w1(3)
-        load_rows(sky_t, sky, 1, "sky")
-        for k in (2, 3):
-            load_rows(page, page0, k, "page")
-            load_rows(sky_t, sky, k, "sky")
+        load_rows(sky_t, sky, [2, 3], "sky")
+        load_rows(page, page0, [4, 5], "page")
+        load_rows(sky_t, sky, [4, 5], "sky")
+        load_rows(page, page0, [6, 7], "page")
 
-        v_w, v_s = [], []
+        v_w, v_s = {}, {}
+
+        def gather_cutout_words(a, tag, calls):
+            v_w[a] = tile([P, S], U32, "v_w%d" % a, tag=tag)
+            width = S // calls
+            for c in range(calls):
+                entries = idx[:, width // 16 * c : width // 16 * (c + 1)]
+                nc.vector.tensor_copy(v_w[a][:, width * c : width * (c + 1)], tab_w[a][:].indirect(entries))
+
+        gather_cutout_words(0, None, 1)
         for a in range(PASSES):
-            s_t = tile([P, S], U8, "v_s%d" % a)
-            nc.vector.tensor_copy(s_t[:], tab_sc[:, T * a : T * (a + 1)].indirect(idx[:]))
-            w_t = tile([P, S], U32, "v_w%d" % a)
-            nc.vector.tensor_copy(w_t[:], tab_w[a][:].indirect(idx[:]))
-            v_s.append(s_t)
-            v_w.append(w_t)
+            v_s[a] = tile([P, S], U8, "v_s%d" % a)
+            nc.vector.tensor_copy(v_s[a][:], tab_sc[:, T * a : T * (a + 1)].indirect(idx[:]))
 
-        for q in range(4):
-            nc.sync.dma_start(
-                tab2_sc[32 * q : 32 * q + 8, :].bitcast(I32),
-                tab2_scales.bitcast(I32)[:, 4 * q : 4 * q + 4, :],
-            )
-        tab2_w = [load_words(tab2_words, a, "tab2_w%d" % a) for a in range(PASSES)]
+        gain_t = tile([P, H // P], F32, "gain_t")
+        gain_bank = ps.tile([P, HALF], F32, name="turn", bufs=4)
+        nc.tensor.transpose(gain_bank[:, :P], gain_rows[:], ident[:])
+        nc.scalar.copy(gain_t[:], gain_bank[:, : H // P])
 
         w1_q = {}
 
-        def quantise_w1(k, cast):
+        def quantise_w1(k, tag, calls, codes_tag=None):
+            grouped = tile([P, PASSES * 4 * PAIR], BF16, "w1_bf%d" % k, tag=tag)
+            codes = tile([P, PASSES * PAIR], U32, "w1_codes%d" % k, tag=codes_tag)
+            scales = tile([P, PASSES * PAIR], U8, "w1_scales%d" % k)
             for a in range(PASSES):
-                grouped = tile([P, 4 * PAIR], BF16, "w1_bf", bufs=4)
-                cast(
-                    grouped[:].rearrange("p (c i j) -> p c j i", i=4, j=4),
+                nc.scalar.copy(
+                    grouped[:, 4 * PAIR * a : 4 * PAIR * (a + 1)].rearrange("p (c i j) -> p c j i", i=4, j=4),
                     w1_raw[k, a][:].rearrange("p j (c i) -> p c j i", i=4),
                 )
-                codes = tile([P, PAIR], U32, "w1_codes%d_%d" % (k, a))
-                scales = tile([P, PAIR], U8, "w1_scales%d_%d" % (k, a))
-                nc.vector.quantize_mx(codes[:].bitcast(FP8X4), scales[:], grouped[:])
-                w1_q[k, a] = (codes, scales)
+            width = PASSES * PAIR // calls
+            for c in range(calls):
+                cols = slice(width * c, width * (c + 1))
+                nc.vector.quantize_mx(
+                    codes[:, cols].bitcast(FP8X4), scales[:, cols], grouped[:, 4 * width * c : 4 * width * (c + 1)]
+                )
+            w1_q[k] = (codes, scales)
 
         def w4_operand(i, a):
             if i < 2:
@@ -155,50 +162,72 @@ def tile_list_lens_arc_scores_kernel(
 
         acc_a, acc_b = {}, {}
 
+        def parts(i):
+            return [slice(0, S // 2), slice(S // 2, S)] if i == 0 else [slice(0, S)]
+
+        def product(i, name, weights):
+            sums = []
+            for n, cols in enumerate(parts(i)):
+                if n == 0:
+                    bank = ps.tile([P, S], F32, name="%s%d" % (name, i % 2))
+                else:
+                    bank = ps.tile([P, HALF], F32, name="turn", bufs=4)
+                acc = bank[:, : cols.stop - cols.start]
+                for a in range(PASSES):
+                    codes, scales = weights(i, a)
+                    nc.tensor.matmul_mx(
+                        acc, codes, scales, v_w[a][:, cols].bitcast(FP8X4), v_s[a][:, cols],
+                        start=(a == 0), stop=(a == PASSES - 1),
+                    )
+                sums.append(acc)
+            return sums
+
+        def w1_operand(i, a):
+            codes, scales = w1_q[i // 2]
+            cols = slice(PAIR * a + P * (i % 2), PAIR * a + P * (i % 2 + 1))
+            return codes[:, cols].bitcast(FP8X4), scales[:, cols]
+
         def first_products(k):
             for i in (2 * k, 2 * k + 1):
-                acc_a[i] = ps.tile([P, S], F32, name="acc_a%d" % (i % 2))
-                for a in range(PASSES):
-                    codes, scales = w1_q[k, a]
-                    cols = slice(P * (i % 2), P * (i % 2 + 1))
-                    nc.tensor.matmul_mx(
-                        acc_a[i][:], codes[:, cols].bitcast(FP8X4), scales[:, cols],
-                        v_w[a][:].bitcast(FP8X4), v_s[a][:], start=(a == 0), stop=(a == PASSES - 1),
-                    )
+                acc_a[i] = product(i, "acc_a", w1_operand)
             for i in (2 * k, 2 * k + 1):
-                acc_b[i] = ps.tile([P, S], F32, name="acc_b%d" % (i % 2))
-                for a in range(PASSES):
-                    words, scales = w4_operand(i, a)
-                    nc.tensor.matmul_mx(
-                        acc_b[i][:], words, scales,
-                        v_w[a][:].bitcast(FP8X4), v_s[a][:], start=(a == 0), stop=(a == PASSES - 1),
-                    )
+                acc_b[i] = product(i, "acc_b", w4_operand)
 
-        h_tags = ["h_even", "h_odd"] * 3 + ["h6", "h7"]
-        h, factor = {}, {}
+        h, factor, squares = {}, {}, {}
 
-        def features(k):
-            pair = (2 * k, 2 * k + 1)
+        def cosine_parts(k):
             sines = tile([P, 2 * S], F32, "sines")
-            squares = tile([P, 2 * S], F32, "squares")
-            for i in pair:
-                cols = slice(S * (i % 2), S * (i % 2 + 1))
-                nc.scalar.activation(sines[:, cols], acc_a[i][:], ACT.Sin, scale=0.5)
-                if k == 0:
-                    nc.scalar.activation(squares[:, cols], sines[:, cols], ACT.Square)
-            if k > 0:
-                nc.scalar.activation(squares[:], sines[:], ACT.Square)
-            factors = tile([P, 2 * S], F32, "factors")
-            u = {}
-            for i in pair:
-                cols = slice(S * (i % 2), S * (i % 2 + 1))
-                factor[i] = factors[:, cols]
+            both = tile([P, 2 * S], F32, "squares%d" % k, tag="squares%d" % (k % 2))
+            for i in (2 * k, 2 * k + 1):
+                mine = slice(S * (i % 2), S * (i % 2 + 1))
+                squares[i] = both[:, mine]
+                for acc, cols in zip(acc_a[i], parts(i)):
+                    nc.scalar.activation(sines[:, mine][:, cols], acc, ACT.Sin, scale=0.5)
+                    if k < 2:
+                        nc.scalar.activation(squares[i][:, cols], sines[:, mine][:, cols], ACT.Square)
+            if k >= 2:
+                nc.scalar.activation(both[:], sines[:], ACT.Square)
+
+        def scale_factors(k):
+            factors = tile([P, 2 * S], F32, "factors%d" % (k % 2))
+            for i in (2 * k, 2 * k + 1):
+                factor[i] = factors[:, S * (i % 2) : S * (i % 2 + 1)]
                 nc.gpsimd.tensor_scalar(factor[i], wgs_t[:], gain_t[:, i : i + 1], 0.0, ALU.mult, ALU.add)
-                u[i] = tile([P, S], F32, "u%d" % (i % 2))
-                nc.vector.scalar_tensor_tensor(u[i][:], squares[:, cols], -0.5, acc_b[i][:], ALU.add, ALU.mult)
-            for i in pair:
-                h[i] = tile([P, S], F32, "h%d" % i, tag=h_tags[i])
-                nc.vector.scalar_tensor_tensor(h[i][:], u[i][:], -2.0, acc_a[i][:], ALU.mult, ALU.add)
+
+        u_slot = ["slot" + c for c in "ABABEDBA"]
+        h_slot = ["slot" + c for c in "CADEABED"]
+
+        u = {}
+
+        def scaled_cosine(i):
+            u[i] = tile([P, S], F32, "u%d" % i, tag=u_slot[i])
+            for acc, cols in zip(acc_b[i], parts(i)):
+                nc.vector.scalar_tensor_tensor(u[i][:, cols], squares[i][:, cols], -0.5, acc, ALU.add, ALU.mult)
+
+        def feature(i):
+            h[i] = tile([P, S], F32, "h%d" % i, tag=h_slot[i])
+            for acc, cols in zip(acc_a[i], parts(i)):
+                nc.vector.scalar_tensor_tensor(h[i][:, cols], u[i][:, cols], -2.0, acc, ALU.mult, ALU.add)
 
         def refresh(i):
             nc.vector.tensor_tensor(page[i][:].indirect(idx3[:]), h[i][:], factor[i], ALU.mult)
@@ -211,11 +240,13 @@ def tile_list_lens_arc_scores_kernel(
                 if ii == 0:
                     x_turned[b, half] = tile([P, 4 * HALF], BF16, "x_turned%d" % half)
                 bank = ps.tile([P, HALF], F32, name="turn", bufs=4)
-                for c in range(4):
-                    cols = slice(HALF * half + P * c, HALF * half + P * (c + 1))
-                    dst = bank[:, P * c : P * (c + 1)]
-                    nc.tensor.matmul(dst, sky_t[i][:, cols], ident[:], start=True, stop=False, is_transpose=True)
-                    nc.tensor.matmul(dst, page[i][:, cols], ident[:], start=False, stop=True, is_transpose=True)
+                for n, term in enumerate((sky_t[i], page[i])):
+                    for c in range(4):
+                        nc.tensor.matmul(
+                            bank[:, P * c : P * (c + 1)], term[:, HALF * half + P * c : HALF * half + P * (c + 1)],
+                            ident[:], start=(n == 0 and c == 0), stop=(n == 1 and c == 3),
+                            is_transpose=True,
+                        )
                 dst = x_turned[b, half][:].rearrange("n (c u p e) -> n c u p e", c=4, u=2, e=2)
                 nc.scalar.copy(
                     dst[:, :, :, 32 * ii : 32 * (ii + 1), :],
@@ -239,25 +270,52 @@ def tile_list_lens_arc_scores_kernel(
                     bank[:].rearrange("p (u n) -> p n u", u=2),
                 )
 
-        def quantise_x(b, half, tag):
-            codes = tile([P, HALF], U32, "x_codes%d_%d" % (b, half), tag=tag)
-            scales = tile([P, HALF], U8, "x_scales%d_%d" % (b, half))
-            nc.vector.quantize_mx(codes[:].bitcast(FP8X4), scales[:], x_grouped[b, half][:])
-            x_q[b, half] = (codes, scales)
+        def quantise_x(b, tag):
+            codes = tile([P, T2], U32, "x_codes%d" % b, tag=tag)
+            scales = tile([P, T2], U8, "x_scales%d" % b)
+            for half in range(2):
+                cols = slice(HALF * half, HALF * (half + 1))
+                nc.vector.quantize_mx(codes[:, cols].bitcast(FP8X4), scales[:, cols], x_grouped[b, half][:])
+                x_q[b, half] = (codes[:, cols], scales[:, cols])
 
-        quantise_w1(0, nc.scalar.copy)
+        quantise_w1(0, "w1_bf0", 2)
+        gather_cutout_words(1, "w1_bf0", 2)
         first_products(0)
-        quantise_w1(1, nc.vector.tensor_copy)
+        idx2 = load_list(offs2, "idx2")
+        p1 = load_list(pos1, "p1")
+        p2 = load_list(pos2, "p2")
+        for q in range(4):
+            nc.sync.dma_start(
+                tab2_sc[32 * q : 32 * q + 8, :].bitcast(I32),
+                tab2_scales.bitcast(I32)[:, 4 * q : 4 * q + 4, :],
+            )
+        tab2_w = [load_words(tab2_words, a, "tab2_w%d" % a) for a in range(PASSES)]
+        load_rows(sky_t, sky, [6, 7], "sky")
+
+        cosine_parts(0)
         for k in range(4):
-            features(k)
+            scale_factors(k)
+            scaled_cosine(2 * k)
+            if k == 0:
+                feature(0)
+                refresh(0)
+                scaled_cosine(1)
+                quantise_w1(1, u_slot[0], 1, h_slot[0])
+            else:
+                scaled_cosine(2 * k + 1)
+                feature(2 * k)
+            feature(2 * k + 1)
             if k < 3:
                 first_products(k + 1)
+            if k > 0:
+                refresh(2 * k)
+            refresh(2 * k + 1)
             if k < 2:
-                quantise_w1(k + 2, nc.scalar.copy)
-            for i in (2 * k, 2 * k + 1):
-                refresh(i)
-                if k == 2:
-                    quantise_x(0, i % 2, h_tags[i])
+                quantise_w1(k + 2, "squares%d" % (k % 2), 1)
+            if k == 2:
+                quantise_x(0, "factors0")
+            if k < 3:
+                cosine_parts(k + 1)
             for i in (2 * k, 2 * k + 1):
                 add_sky(i)
             if k % 2 == 1:
@@ -270,7 +328,7 @@ def tile_list_lens_arc_scores_kernel(
             nc.sync.dma_start(t[:], low[PAIR * m2 : PAIR * (m2 + 1), :].rearrange("(m p) j -> p m j", p=P))
             low_t.append(t)
 
-        v2_s = tile([P, S2], U8, "v2_s", tag="h7")
+        v2_s = tile([P, S2], U8, "v2_s", tag=h_slot[7])
         nc.vector.tensor_copy(v2_s[:], tab2_sc[:].indirect(idx2[:]))
 
         def gather_candidates(part, tag):
@@ -281,9 +339,8 @@ def tile_list_lens_arc_scores_kernel(
                 )
             return t
 
-        v2_w = [gather_candidates(0, "factors")]
-        for half in range(2):
-            quantise_x(1, half, None)
+        v2_w = [gather_candidates(0, "factors1")]
+        quantise_x(1, None)
         v2_w.append(gather_candidates(1, "x_grouped1"))
 
         for m in range(S2 // P):
@@ -296,17 +353,18 @@ def tile_list_lens_arc_scores_kernel(
                     nc.tensor.matmul_mx(
                         bank[:], v2_w[m // 4][:, first : first + P].bitcast(FP8X4),
                         v2_s[4 * a : P, P * m : P * (m + 1)],
-                        codes[:].bitcast(FP8X4), scales[:], start=(a == 0), stop=(a == PASSES - 1),
+                        codes.bitcast(FP8X4), scales, start=(a == 0), stop=(a == PASSES - 1),
                     )
                 nc.scalar.copy(scores[:, HALF * half : HALF * (half + 1)], bank[:])
             second = tile([P, NP], F32, "second", bufs=2)
             arcs = tile([P, NP], F32, "arcs", bufs=2)
             result = tile([P, NP], F32, "result", bufs=3)
-            parts = [(slice(16 * c, 16 * (c + 1)), slice(PAIR * c, PAIR * (c + 1))) for c in range(2)]
-            for entries, cols in parts:
+            halves = [(slice(16 * c, 16 * (c + 1)), slice(PAIR * c, PAIR * (c + 1))) for c in range(2)]
+            for entries, cols in halves:
                 nc.vector.tensor_copy(second[:, cols], scores[:].indirect(p2[:, entries]))
-            for entries, cols in parts:
+            for entries, cols in halves:
                 nc.vector.tensor_tensor(arcs[:, cols], scores[:].indirect(p1[:, entries]), second[:, cols], ALU.subtract)
-            for entries, cols in parts:
+            for entries, cols in halves:
                 nc.vector.tensor_tensor(result[:, cols], arcs[:, cols], low_t[m // 2][:, m % 2, cols], ALU.max)
-            nc.sync.dma_start(out[P * m : P * (m + 1), :], result[:])
+            for cols in [cols for entries, cols in halves] if m == S2 // P - 1 else [slice(0, NP)]:
+                nc.sync.dma_start(out[P * m : P * (m + 1), cols], result[:, cols])

from contextlib import ExitStack

import concourse.mybir as mybir
from concourse.masks import make_identity

K, T, S, H, S2, T3, T2, NP = 1024, 2048, 512, 1024, 1024, 2048, 1024, 512
FLOPS = 2 * 2 * K * H * S + 2 * H * S2 * T2

F32 = mybir.dt.float32
BF16 = mybir.dt.bfloat16
I32 = mybir.dt.int32
U32 = mybir.dt.uint32
U16 = mybir.dt.uint16
U8 = mybir.dt.uint8
FP8X4 = mybir.dt.float8_e4m3fn_x4
FP4X4 = mybir.dt.float4_e2m1fn_x4
ALU = mybir.AluOpType
ACT = mybir.ActivationFunctionType

P = 128
PASSES = 2
PAIR = 2 * P
HALF = 512


def tile_list_lens_arc_scores_kernel(
    tc, tab_words, tab_scales, offs, tab2_words, tab2_scales, offs2, offs3, pos1, pos2,
    w1, w4_words, w4_scales, gain, wgs, page0, sky, low, out,
):
    nc = tc.nc
    with ExitStack() as ctx:
        lists = ctx.enter_context(tc.tile_pool(name="lists", bufs=1))
        sb = ctx.enter_context(tc.tile_pool(name="sb", bufs=1))
        ps = ctx.enter_context(tc.psum_pool(name="ps", bufs=1))

        def tile(shape, dtype, name, tag=None, bufs=1):
            return sb.tile(shape, dtype, name=name, tag=tag or name, bufs=bufs, align_bytes=64)

        def load_list(ap, name):
            t = lists.tile(list(ap.shape), U16, name=name)
            nc.sync.dma_start(t[:], ap)
            return t

        tab_sc = tile([P, PASSES * T], U8, "tab_sc")
        nc.gpsimd.memset(tab_sc[:, :T].bitcast(I32), 0)
        nc.vector.memset(tab_sc[:, T:].bitcast(I32), 0)
        w4_sc = tile([P, PASSES * H], U8, "w4_sc")
        nc.vector.memset(w4_sc[:].bitcast(I32), 0)
        tab2_sc = tile([P, T3], U8, "tab2_sc")
        nc.vector.memset(tab2_sc[:].bitcast(I32), 0)
        ident = tile([P, P], F32, "ident")
        make_identity(nc, ident[:])
        gain_rows = tile([P, P], F32, "gain_rows")
        nc.gpsimd.memset(gain_rows[:], 0.0)

        def load_words(words, a, name):
            t = tile([P, T], U32, name, tag="words%d" % a)
            nc.sync.dma_start(t[:].bitcast(I32), words[a].rearrange("p n t -> p (n t)").bitcast(I32))
            return t

        def load_scales_side_by_side(dst, scales):
            for q in range(4):
                nc.sync.dma_start(
                    dst[32 * q : 32 * q + 4, :].bitcast(I32).rearrange("q (a t) -> q a t", a=PASSES),
                    scales.bitcast(I32)[:, 4 * q : 4 * q + 4, :].rearrange("a q t -> q a t"),
                )

        w1_raw = {}

        def load_w1(k, passes=(0, 1)):
            for a in passes:
                t = tile([P, 4, PAIR], F32, "w1_raw%d_%d" % (k, a))
                src = w1[512 * a : 512 * (a + 1), PAIR * k : PAIR * (k + 1)]
                nc.sync.dma_start(t[:], src.rearrange("(p j) c -> p j c", j=4))
                w1_raw[k, a] = t

        def load_w4(c0, c1, name):
            t = tile([P, PASSES, 2 * (c1 - c0)], U8, name)
            nc.sync.dma_start(
                t[:].bitcast(I32),
                w4_words.bitcast(I32)[:, :, c0 // 2 : c1 // 2].rearrange("a p c -> p a c"),
            )
            return t

        page, sky_t = {}, {}

        def load_rows(dst, src, tiles, name):
            for i in tiles:
                t = tile([P, T2], F32, "%s%d" % (name, i))
                nc.sync.dma_start(t[:], src[P * i : P * (i + 1), :])
                dst[i] = t

        idx = load_list(offs, "idx")
        tab_w = [load_words(tab_words, 0, "tab_w0")]
        load_scales_side_by_side(tab_sc, tab_scales)
        nc.sync.dma_start(gain_rows[: H // P, :], gain.rearrange("(i p) -> i p", p=P))
        load_w1(0, (0,))
        w4_first = load_w4(0, PAIR, "w4_first")
        load_w1(0, (1,))
        tab_w.append(load_words(tab_words, 1, "tab_w1"))
        load_scales_side_by_side(w4_sc, w4_scales)
        wgs_t = tile([P, S], F32, "wgs_t")
        nc.sync.dma_start(wgs_t[:], wgs)
        load_rows(page, page0, [0], "page")
        idx3 = load_list(offs3, "idx3")
        load_w1(1)
        load_rows(page, page0, [1], "page")
        w4_rest = load_w4(PAIR, H, "w4_rest")
        load_w1(2)
        load_rows(sky_t, sky, [0, 1], "sky")
        load_rows(page, page0, [2, 3], "page")
        load_w1(3)
        load_rows(sky_t, sky, [2, 3], "sky")
        load_rows(page, page0, [4, 5], "page")
        load_rows(sky_t, sky, [4, 5], "sky")
        load_rows(page, page0, [6, 7], "page")

        v_w, v_s = {}, {}

        def gather_cutout_words(a, tag, calls):
            v_w[a] = tile([P, S], U32, "v_w%d" % a, tag=tag)
            width = S // calls
            for c in range(calls):
                entries = idx[:, width // 16 * c : width // 16 * (c + 1)]
                nc.vector.tensor_copy(v_w[a][:, width * c : width * (c + 1)], tab_w[a][:].indirect(entries))

        gather_cutout_words(0, None, 1)
        for a in range(PASSES):
            v_s[a] = tile([P, S], U8, "v_s%d" % a)
            nc.vector.tensor_copy(v_s[a][:], tab_sc[:, T * a : T * (a + 1)].indirect(idx[:]))

        gain_t = tile([P, H // P], F32, "gain_t")
        gain_bank = ps.tile([P, HALF], F32, name="turn", bufs=4)
        nc.tensor.transpose(gain_bank[:, :P], gain_rows[:], ident[:])
        nc.scalar.copy(gain_t[:], gain_bank[:, : H // P])

        w1_q = {}

        def quantise_w1(k, tag, calls, codes_tag=None):
            grouped = tile([P, PASSES * 4 * PAIR], BF16, "w1_bf%d" % k, tag=tag)
            codes = tile([P, PASSES * PAIR], U32, "w1_codes%d" % k, tag=codes_tag)
            scales = tile([P, PASSES * PAIR], U8, "w1_scales%d" % k)
            for a in range(PASSES):
                nc.scalar.copy(
                    grouped[:, 4 * PAIR * a : 4 * PAIR * (a + 1)].rearrange("p (c i j) -> p c j i", i=4, j=4),
                    w1_raw[k, a][:].rearrange("p j (c i) -> p c j i", i=4),
                )
            width = PASSES * PAIR // calls
            for c in range(calls):
                cols = slice(width * c, width * (c + 1))
                nc.vector.quantize_mx(
                    codes[:, cols].bitcast(FP8X4), scales[:, cols], grouped[:, 4 * width * c : 4 * width * (c + 1)]
                )
            w1_q[k] = (codes, scales)

        def w4_operand(i, a):
            if i < 2:
                words = w4_first[:, a, 2 * P * i : 2 * P * (i + 1)]
            else:
                words = w4_rest[:, a, 2 * P * (i - 2) : 2 * P * (i - 1)]
            return words.bitcast(FP4X4), w4_sc[:, H * a + P * i : H * a + P * (i + 1)]

        acc_a, acc_b = {}, {}

        def parts(i):
            return [slice(0, S // 2), slice(S // 2, S)] if i == 0 else [slice(0, S)]

        def product(i, name, weights):
            sums = []
            for n, cols in enumerate(parts(i)):
                if n == 0:
                    bank = ps.tile([P, S], F32, name="%s%d" % (name, i % 2))
                else:
                    bank = ps.tile([P, HALF], F32, name="turn", bufs=4)
                acc = bank[:, : cols.stop - cols.start]
                for a in range(PASSES):
                    codes, scales = weights(i, a)
                    nc.tensor.matmul_mx(
                        acc, codes, scales, v_w[a][:, cols].bitcast(FP8X4), v_s[a][:, cols],
                        start=(a == 0), stop=(a == PASSES - 1),
                    )
                sums.append(acc)
            return sums

        def w1_operand(i, a):
            codes, scales = w1_q[i // 2]
            cols = slice(PAIR * a + P * (i % 2), PAIR * a + P * (i % 2 + 1))
            return codes[:, cols].bitcast(FP8X4), scales[:, cols]

        def first_products(k):
            for i in (2 * k, 2 * k + 1):
                acc_a[i] = product(i, "acc_a", w1_operand)
            for i in (2 * k, 2 * k + 1):
                acc_b[i] = product(i, "acc_b", w4_operand)

        h, factor, squares = {}, {}, {}

        def cosine_parts(k):
            sines = tile([P, 2 * S], F32, "sines")
            both = tile([P, 2 * S], F32, "squares%d" % k, tag="squares%d" % (k % 2))
            for i in (2 * k, 2 * k + 1):
                mine = slice(S * (i % 2), S * (i % 2 + 1))
                squares[i] = both[:, mine]
                for acc, cols in zip(acc_a[i], parts(i)):
                    nc.scalar.activation(sines[:, mine][:, cols], acc, ACT.Sin, scale=0.5)
                    if k < 2:
                        nc.scalar.activation(squares[i][:, cols], sines[:, mine][:, cols], ACT.Square)
            if k >= 2:
                nc.scalar.activation(both[:], sines[:], ACT.Square)

        def scale_factors(k):
            factors = tile([P, 2 * S], F32, "factors%d" % (k % 2))
            for i in (2 * k, 2 * k + 1):
                factor[i] = factors[:, S * (i % 2) : S * (i % 2 + 1)]
                nc.gpsimd.tensor_scalar(factor[i], wgs_t[:], gain_t[:, i : i + 1], 0.0, ALU.mult, ALU.add)

        u_slot = ["slot" + c for c in "ABABEDBA"]
        h_slot = ["slot" + c for c in "CADEABED"]

        u = {}

        def scaled_cosine(i):
            u[i] = tile([P, S], F32, "u%d" % i, tag=u_slot[i])
            for acc, cols in zip(acc_b[i], parts(i)):
                nc.vector.scalar_tensor_tensor(u[i][:, cols], squares[i][:, cols], -0.5, acc, ALU.add, ALU.mult)

        def feature(i):
            h[i] = tile([P, S], F32, "h%d" % i, tag=h_slot[i])
            for acc, cols in zip(acc_a[i], parts(i)):
                nc.vector.scalar_tensor_tensor(h[i][:, cols], u[i][:, cols], -2.0, acc, ALU.mult, ALU.add)

        def refresh(i):
            nc.vector.tensor_tensor(page[i][:].indirect(idx3[:]), h[i][:], factor[i], ALU.mult)

        x_turned, x_grouped, x_q = {}, {}, {}

        def add_sky(i):
            b, ii = divmod(i, 4)
            for half in range(2):
                if ii == 0:
                    x_turned[b, half] = tile([P, 4 * HALF], BF16, "x_turned%d" % half)
                bank = ps.tile([P, HALF], F32, name="turn", bufs=4)
                for n, term in enumerate((sky_t[i], page[i])):
                    for c in range(4):
                        nc.tensor.matmul(
                            bank[:, P * c : P * (c + 1)], term[:, HALF * half + P * c : HALF * half + P * (c + 1)],
                            ident[:], start=(n == 0 and c == 0), stop=(n == 1 and c == 3),
                            is_transpose=True,
                        )
                dst = x_turned[b, half][:].rearrange("n (c u p e) -> n c u p e", c=4, u=2, e=2)
                nc.scalar.copy(
                    dst[:, :, :, 32 * ii : 32 * (ii + 1), :],
                    bank[:].rearrange("n (c p u e) -> n c u p e", c=4, u=2, e=2),
                )

        def turn_back(b, half):
            x_grouped[b, half] = tile([P, 4 * HALF], BF16, "x_grouped%d" % half)
            pairs = x_turned[b, half][:].bitcast(F32)
            dst = x_grouped[b, half][:].bitcast(F32)
            for g in range(2):
                bank = ps.tile([P, HALF], F32, name="turn", bufs=4)
                for u in range(2):
                    for c in range(2):
                        first = P * (2 * (2 * g + c) + u)
                        nc.tensor.transpose(
                            bank[:, PAIR * u + P * c : PAIR * u + P * (c + 1)], pairs[:, first : first + P], ident[:]
                        )
                nc.scalar.copy(
                    dst[:, HALF * g : HALF * (g + 1)].rearrange("p (n u) -> p n u", u=2),
                    bank[:].rearrange("p (u n) -> p n u", u=2),
                )

        def quantise_x(b, tag):
            codes = tile([P, T2], U32, "x_codes%d" % b, tag=tag)
            scales = tile([P, T2], U8, "x_scales%d" % b)
            for half in range(2):
                cols = slice(HALF * half, HALF * (half + 1))
                nc.vector.quantize_mx(codes[:, cols].bitcast(FP8X4), scales[:, cols], x_grouped[b, half][:])
                x_q[b, half] = (codes[:, cols], scales[:, cols])

        quantise_w1(0, "w1_bf0", 2)
        gather_cutout_words(1, "w1_bf0", 2)
        first_products(0)
        idx2 = load_list(offs2, "idx2")
        p1 = load_list(pos1, "p1")
        p2 = load_list(pos2, "p2")
        for q in range(4):
            nc.sync.dma_start(
                tab2_sc[32 * q : 32 * q + 8, :].bitcast(I32),
                tab2_scales.bitcast(I32)[:, 4 * q : 4 * q + 4, :],
            )
        tab2_w = [load_words(tab2_words, a, "tab2_w%d" % a) for a in range(PASSES)]
        load_rows(sky_t, sky, [6, 7], "sky")

        cosine_parts(0)
        for k in range(4):
            scale_factors(k)
            scaled_cosine(2 * k)
            if k == 0:
                feature(0)
                refresh(0)
                scaled_cosine(1)
                quantise_w1(1, u_slot[0], 1, h_slot[0])
            else:
                scaled_cosine(2 * k + 1)
                feature(2 * k)
            feature(2 * k + 1)
            if k < 3:
                first_products(k + 1)
            if k > 0:
                refresh(2 * k)
            refresh(2 * k + 1)
            if k < 2:
                quantise_w1(k + 2, "squares%d" % (k % 2), 1)
            if k == 2:
                quantise_x(0, "factors0")
            if k < 3:
                cosine_parts(k + 1)
            for i in (2 * k, 2 * k + 1):
                add_sky(i)
            if k % 2 == 1:
                for half in range(2):
                    turn_back(k // 2, half)

        low_t = []
        for m2 in range(4):
            t = tile([P, 2, NP], F32, "low%d" % m2, tag="w1_raw%d_%d" % divmod(m2, 2))
            nc.sync.dma_start(t[:], low[PAIR * m2 : PAIR * (m2 + 1), :].rearrange("(m p) j -> p m j", p=P))
            low_t.append(t)

        v2_s = tile([P, S2], U8, "v2_s", tag=h_slot[7])
        nc.vector.tensor_copy(v2_s[:], tab2_sc[:].indirect(idx2[:]))

        def gather_candidates(part, tag):
            t = tile([P, PASSES * HALF], U32, "v2_w%d" % part, tag=tag)
            for a in range(PASSES):
                nc.vector.tensor_copy(
                    t[:, HALF * a : HALF * (a + 1)], tab2_w[a][:].indirect(idx2[:, 32 * part : 32 * (part + 1)])
                )
            return t

        v2_w = [gather_candidates(0, "factors1")]
        quantise_x(1, None)
        v2_w.append(gather_candidates(1, "x_grouped1"))

        for m in range(S2 // P):
            scores = tile([P, T2], F32, "scores%d" % m, tag="sky%d" % m)
            for half in range(2):
                bank = ps.tile([P, HALF], F32, name="turn", bufs=4)
                for a in range(PASSES):
                    first = HALF * a + P * (m % 4)
                    codes, scales = x_q[a, half]
                    nc.tensor.matmul_mx(
                        bank[:], v2_w[m // 4][:, first : first + P].bitcast(FP8X4),
                        v2_s[4 * a : P, P * m : P * (m + 1)],
                        codes.bitcast(FP8X4), scales, start=(a == 0), stop=(a == PASSES - 1),
                    )
                nc.scalar.copy(scores[:, HALF * half : HALF * (half + 1)], bank[:])
            second = tile([P, NP], F32, "second", bufs=2)
            arcs = tile([P, NP], F32, "arcs", bufs=2)
            result = tile([P, NP], F32, "result", bufs=3)
            halves = [(slice(16 * c, 16 * (c + 1)), slice(PAIR * c, PAIR * (c + 1))) for c in range(2)]
            for entries, cols in halves:
                nc.vector.tensor_copy(second[:, cols], scores[:].indirect(p2[:, entries]))
            for entries, cols in halves:
                nc.vector.tensor_tensor(arcs[:, cols], scores[:].indirect(p1[:, entries]), second[:, cols], ALU.subtract)
            for entries, cols in halves:
                nc.vector.tensor_tensor(result[:, cols], arcs[:, cols], low_t[m // 2][:, m % 2, cols], ALU.max)
            for cols in [cols for entries, cols in halves] if m == S2 // P - 1 else [slice(0, NP)]:
                nc.sync.dma_start(out[P * m : P * (m + 1), cols], result[:, cols])
